import numpy as np
import ml_dtypes


def mxq(x, axis, fmt="e4m3"):
    dtype, down = {"e4m3": (ml_dtypes.float8_e4m3fn, 7), "e5m2": (ml_dtypes.float8_e5m2, 14)}[fmt]
    v = np.moveaxis(np.asarray(x, np.float32).astype(ml_dtypes.bfloat16).astype(np.float64), axis, -1)
    blocks = v.reshape(v.shape[:-1] + (-1, 32))
    amax = np.abs(blocks).max(-1, keepdims=True)
    byte = np.maximum(np.where(amax > 0, np.frexp(amax)[1] - 1 + 127, 0) - down, 1)
    scale = np.exp2(byte - 127.0)
    codes = (blocks / scale).astype(np.float32).astype(dtype).astype(np.float64)
    return np.moveaxis((codes * scale).reshape(v.shape), -1, axis)


WIDE = False


def mx_kscale(k):
    if not WIDE:
        return np.ones(k)
    levels = np.array([30, -30])
    if k % 512:
        return np.exp2(np.random.permutation(np.resize(levels, k // 32))).repeat(32)
    a = np.empty((k // 512, 16))
    for p in range(k // 512):
        a[p, :8] = np.random.permutation(np.resize(levels, 8))
        for g in range(8):
            far = levels[np.abs(levels - a[p, g]) >= 10]
            a[p, g + 8] = far[np.random.randint(len(far))]
    return np.exp2(a.ravel()).repeat(32)


def f64(x):
    return np.asarray(x).astype(np.float64)


def striped(idx):
    return np.tile(np.asarray(idx).reshape(-1, 16).T, (8, 1)).astype(np.uint16)


def unstriped(offs):
    return offs[:16].T.reshape(-1).astype(np.int64)


E2M1 = np.array([0.0, 0.5, 1.0, 1.5, 2.0, 3.0, 4.0, 6.0, -0.0, -0.5, -1.0, -1.5, -2.0, -3.0, -4.0, -6.0])


def pack_weight(w, fmt):
    k, n = w.shape
    w = f64(np.asarray(w, np.float32).astype(ml_dtypes.bfloat16)).reshape(k // 32, 32, n)
    amax = np.abs(w).max(1)
    if fmt == "e4m3":
        byte = np.frexp(amax)[1] - 1 + 127 - 7
    else:
        mant, ex = np.frexp(amax / 6.0)
        byte = np.where(mant > 0.5, ex, ex - 1) + 127
    byte = np.clip(np.where(amax > 0, byte, 1), 1, 254)
    scaled = (w * np.exp2(127.0 - byte)[:, None, :]).reshape(k, n).astype(np.float32)
    by_word = np.ascontiguousarray(scaled.reshape(k // 512, 128, 4, n).transpose(0, 1, 3, 2))
    if fmt == "e4m3":
        words = by_word.astype(ml_dtypes.float8_e4m3fn).view(np.uint8)
    else:
        c = by_word.astype(ml_dtypes.float4_e2m1fn).view(np.uint8) & 0xF
        words = (c[..., 0::2] | (c[..., 1::2] << 4)).reshape(k // 512, 128, 2 * n)
    return np.ascontiguousarray(words), np.ascontiguousarray(byte.astype(np.uint8).reshape(k // 512, 16, n))


def unpack_weight(words, scales, fmt):
    g, _, n = scales.shape
    words = np.ascontiguousarray(words).reshape(g, 128, n, -1)
    if fmt == "e4m3":
        vals = words.view(ml_dtypes.float8_e4m3fn).astype(np.float64)
    else:
        nib = np.empty((g, 128, n, 4), np.uint8)
        nib[..., 0::2] = words & 0xF
        nib[..., 1::2] = words >> 4
        vals = E2M1[nib]
    vals = vals * np.repeat(np.exp2(scales.astype(np.float64) - 127.0), 8, axis=1)[..., None]
    return vals.transpose(0, 1, 3, 2).reshape(g * 512, n)


K, T, J, S, R, V, N = 1024, 1024, 256, 512, 512, 512, 256


def setup_inputs():
    n = np.random.standard_normal
    idx = np.random.permutation(T)[:J]
    idx2 = np.random.permutation(S)[:J]
    idx3 = np.random.permutation(V)[:J]
    fk = mx_kscale(K)
    fr = mx_kscale(R)
    wp = pack_weight(n((K, R)) * 1 / np.sqrt(K) * fk[:, None] * fr, "e2m1")
    wbp = pack_weight(n((R, N)) * 1 / np.sqrt(R) / fr[:, None], "e4m3")
    return {
        "xa": (n((K, T))).astype(np.float32),
        "xb": (n((K, S))).astype(np.float32),
        "hb": (np.random.uniform(0.2, 0.9, (K, 1))).astype(np.float32),
        "fk": (np.random.uniform(0.5, 2.0, (K, 1)) / fk[:, None]).astype(np.float32),
        "w_words": wp[0],
        "w_scales": wp[1],
        "tb": (n((R, V)) * 0.7 * fr[:, None]).astype(np.float32),
        "wb_words": wbp[0],
        "wb_scales": wbp[1],
        "rs": (1.0 * n((J, N))).astype(np.float32),
        "offs": striped(idx),
        "offs2": striped(idx2),
        "offs3": striped(idx3),
    }


def reference(xa, xb, hb, fk, w_words, w_scales, tb, wb_words, wb_scales, rs, offs, offs2, offs3):
    idx = unstriped(offs)
    idx2 = unstriped(offs2)
    idx3 = unstriped(offs3)
    wu = unpack_weight(w_words, w_scales, "e2m1")
    wbu = unpack_weight(wb_words, wb_scales, "e4m3")
    u = (f64(xa)[:, idx] - np.minimum(f64(xb)[:, idx2], f64(hb))) * f64(fk)
    uq = mxq(u, 0, "e4m3")
    a = wu.T @ uq
    hid = np.maximum(a - f64(tb)[:, idx3], 0.0)
    hidq = mxq(hid, 0, "e5m2")
    p = hidq.T @ wbu
    pk2 = np.max(np.abs(p), axis=1, keepdims=True)
    y = p / (pk2 + 0.2) + 0.3 * f64(rs)
    return y

@@ -1,0 +1,188 @@
+from contextlib import ExitStack
+
+import concourse.mybir as mybir
+
+K, T, J, S, R, V, N = 1024, 1024, 256, 512, 512, 512, 256
+FLOPS = 2 * K * R * J + 2 * R * J * N
+
+F32 = mybir.dt.float32
+BF16 = mybir.dt.bfloat16
+I32 = mybir.dt.int32
+U32 = mybir.dt.uint32
+U16 = mybir.dt.uint16
+U8 = mybir.dt.uint8
+E4M3 = mybir.dt.float8_e4m3fn_x4
+E5M2 = mybir.dt.float8_e5m2_x4
+E2M1 = mybir.dt.float4_e2m1fn_x4
+ALU = mybir.AluOpType
+ACT = mybir.ActivationFunctionType
+
+P = 128
+PACK = 4
+PASSES = K // (P * PACK)
+HALVES = J // P
+LIST_COLS = J // 16
+HALF_COLS = P // 16
+
+
+def tile_list_boundedgaps_overtable_rowpeaks_kernel(
+    tc, xa, xb, hb, fk, w_words, w_scales, tb, wb_words, wb_scales, rs, offs, offs2, offs3, out
+):
+    nc = tc.nc
+    with ExitStack() as ctx:
+        keep = ctx.enter_context(tc.tile_pool(name="keep", bufs=1))
+        psum = ctx.enter_context(tc.psum_pool(name="psum", bufs=1))
+
+        xa_v = xa.rearrange("(a p t) c -> a p t c", a=PASSES, p=P, t=PACK)
+        xb_v = xb.rearrange("(a p t) c -> a p t c", a=PASSES, p=P, t=PACK)
+        tb_v = tb.rearrange("(p t) c -> p t c", p=P, t=PACK)
+
+        list_a = keep.tile([P, LIST_COLS], U16, name="list_a")
+        list_b = keep.tile([P, LIST_COLS], U16, name="list_b")
+        list_t = keep.tile([P, LIST_COLS], U16, name="list_t")
+        hb_sb = keep.tile([P, PASSES, PACK], F32, name="hb_sb")
+        fk_sb = keep.tile([P, PASSES, PACK], F32, name="fk_sb")
+        w_raw = keep.tile([P, PASSES, 2 * R], U8, name="w_raw", align_bytes=64)
+        w_codes = keep.tile([P, PASSES, 2 * R], U8, name="w_codes", align_bytes=64)
+        ws_raw = keep.tile([P, PASSES, R], U8, name="ws_raw", align_bytes=64)
+        ws_sb = keep.tile([P, PASSES, R], U8, name="ws_sb", align_bytes=64)
+        wb_codes = keep.tile([P, N], U32, name="wb_codes", align_bytes=64)
+        wbs_sb = keep.tile([P, N], U8, name="wbs_sb", align_bytes=64)
+        rs_sb = keep.tile([P, HALVES, N], F32, name="rs_sb")
+
+        def load_planes(name, view, t0, t1):
+            tile = keep.tile([P, t1 - t0, view.shape[2]], F32, name=name)
+            nc.sync.dma_start(out=tile[:], in_=view[:, t0:t1, :])
+            return [tile[:, t - t0, :] for t in range(t0, t1)]
+
+        nc.scalar.dma_start(out=hb_sb[:], in_=hb.rearrange("(a p t) o -> p a (t o)", a=PASSES, p=P, t=PACK))
+        nc.scalar.dma_start(out=fk_sb[:], in_=fk.rearrange("(a p t) o -> p a (t o)", a=PASSES, p=P, t=PACK))
+        nc.sync.dma_start(list_b[:], offs2)
+        xb_planes = [load_planes("xb0", xb_v[0], 0, 4)]
+        nc.sync.dma_start(list_a[:], offs)
+        nc.sync.dma_start(out=w_raw[:].bitcast(I32), in_=w_words.rearrange("a p c -> p a c").bitcast(I32))
+        xa_planes = [load_planes("xa00", xa_v[0], 0, 2) + load_planes("xa02", xa_v[0], 2, 4)]
+        nc.sync.dma_start(list_t[:], offs3)
+        xb_planes.append(load_planes("xb1", xb_v[1], 0, 4))
+        xa_planes.append(
+            load_planes("xa10", xa_v[1], 0, 2) + load_planes("xa12", xa_v[1], 2, 3) + load_planes("xa13", xa_v[1], 3, 4)
+        )
+        tb_planes = load_planes("tb0", tb_v, 0, 2) + load_planes("tb2", tb_v, 2, 3) + load_planes("tb3", tb_v, 3, 4)
+        nc.sync.dma_start(out=wb_codes[:].bitcast(I32), in_=wb_words[0].rearrange("p n t -> p (n t)").bitcast(I32))
+        nc.sync.dma_start(out=rs_sb[:], in_=rs.rearrange("(h p) n -> p h n", p=P))
+
+        nc.gpsimd.memset(ws_raw[:].bitcast(I32), 0)
+        nc.gpsimd.memset(wbs_sb[:].bitcast(I32), 0)
+        for q in range(4):
+            nc.gpsimd.dma_start(
+                out=ws_raw[32 * q : 32 * q + 4, :, :].bitcast(I32),
+                in_=w_scales[:, 4 * q : 4 * q + 4, :].rearrange("a r c -> r a c").bitcast(I32),
+            )
+        for q in range(4):
+            nc.gpsimd.dma_start(
+                out=wbs_sb[32 * q : 32 * q + 4, :].bitcast(I32),
+                in_=wb_scales[0, 4 * q : 4 * q + 4, :].bitcast(I32),
+            )
+
+        nc.vector.tensor_copy(
+            out=w_codes[:].bitcast(U16).rearrange("p a (t m) -> p a t m", t=PACK),
+            in_=w_raw[:].bitcast(U16).rearrange("p a (m t) -> p a t m", t=PACK),
+        )
+        nc.vector.tensor_copy(
+            out=ws_sb[:].rearrange("p a (t m) -> p a t m", t=PACK),
+            in_=ws_raw[:].rearrange("p a (m t) -> p a t m", t=PACK),
+        )
+
+        def gather(dst, window, offsets, by_halves):
+            if by_halves:
+                for h in range(HALVES):
+                    part = offsets[:, h * HALF_COLS : (h + 1) * HALF_COLS]
+                    nc.scalar.activation(dst[:, h * P : (h + 1) * P], window.indirect(part), ACT.Copy)
+            else:
+                nc.scalar.activation(dst, window.indirect(offsets[:]), ACT.Copy)
+
+        a_ps = [psum.tile([P, PACK, P], F32, name="a_ps%d" % h) for h in range(HALVES)]
+        for a in range(PASSES):
+            ga = keep.tile([P, PACK, J], F32, name="ga%d" % a)
+            gb = keep.tile([P, PACK, J], F32, name="gb%d" % a)
+            gap = keep.tile([P, PACK, J], F32, name="gap%d" % a)
+            u_bf = keep.tile([P, J, PACK], BF16, name="u_bf%d" % a, align_bytes=64)
+            u_codes = keep.tile([P, J], U32, name="u_codes%d" % a, align_bytes=64)
+            u_scales = keep.tile([P, J], U8, name="u_scales%d" % a, align_bytes=64)
+            for t in range(PACK):
+                gather(gb[:, t, :], xb_planes[a][t], list_b, False)
+            for t in range(PACK):
+                last = a == PASSES - 1 and t == PACK - 1
+                gather(ga[:, t, :], xa_planes[a][t], list_a, last)
+                spans = [slice(h * P, (h + 1) * P) for h in range(HALVES)] if last else [slice(0, J)]
+                for js in spans:
+                    nc.vector.scalar_tensor_tensor(
+                        out=gap[:, t, js], in0=gb[:, t, js], scalar=hb_sb[:, a, t : t + 1], in1=ga[:, t, js],
+                        op0=ALU.min, op1=ALU.subtract,
+                    )
+                for js in spans:
+                    nc.vector.tensor_scalar(
+                        out=u_bf[:, js, t], in0=gap[:, t, js], scalar1=fk_sb[:, a, t : t + 1], scalar2=-1.0,
+                        op0=ALU.mult, op1=ALU.mult,
+                    )
+            for h in range(HALVES):
+                js = slice(h * P, (h + 1) * P)
+                nc.vector.quantize_mx(
+                    out=u_codes[:, js].bitcast(E4M3), scales=u_scales[:, js],
+                    in_=u_bf[:, js, :].rearrange("p j t -> p (j t)"),
+                )
+            for h in range(HALVES):
+                js = slice(h * P, (h + 1) * P)
+                for t in range(PACK):
+                    nc.tensor.matmul_mx(
+                        out=a_ps[h][:, t, :],
+                        lhsT=w_codes[:, a, 2 * P * t : 2 * P * (t + 1)].bitcast(E2M1),
+                        lhsT_scale=ws_sb[:, a, P * t : P * (t + 1)],
+                        rhs=u_codes[:, js].bitcast(E4M3),
+                        rhs_scale=u_scales[:, js],
+                        start=(a == 0 and t == 0),
+                        stop=(a == PASSES - 1 and t == PACK - 1),
+                    )
+
+        gt = keep.tile([P, PACK, J], F32, name="gt")
+        for t in range(PACK):
+            gather(gt[:, t, :], tb_planes[t], list_t, t == PACK - 1)
+        rs_scaled = keep.tile([P, HALVES, N], F32, name="rs_scaled")
+        nc.scalar.activation(rs_scaled[:], rs_sb[:], ACT.Copy, scale=0.3)
+
+        pre = [keep.tile([P, P * PACK], BF16, name="pre%d" % h, align_bytes=64) for h in range(HALVES)]
+        hid = [keep.tile([P, P * PACK], BF16, name="hid%d" % h, align_bytes=64) for h in range(HALVES)]
+        h_codes = [keep.tile([P, P], U32, name="h_codes%d" % h, align_bytes=64) for h in range(HALVES)]
+        h_scales = [keep.tile([P, P], U8, name="h_scales%d" % h, align_bytes=64) for h in range(HALVES)]
+        p_ps = [psum.tile([P, N], F32, name="p_ps%d" % h) for h in range(HALVES)]
+        mag = [keep.tile([P, N], F32, name="mag%d" % h) for h in range(HALVES)]
+        den = [keep.tile([P, 1], F32, name="den%d" % h) for h in range(HALVES)]
+        inv = [keep.tile([P, 1], F32, name="inv%d" % h) for h in range(HALVES)]
+        res = [keep.tile([P, N], F32, name="res%d" % h) for h in range(HALVES)]
+        for h in range(HALVES):
+            nc.vector.tensor_tensor(
+                out=pre[h][:].rearrange("p (c i t) -> p c t i", i=4, t=PACK),
+                in0=a_ps[h][:].rearrange("p t (c i) -> p c t i", i=4),
+                in1=gt[:, :, h * P : (h + 1) * P].rearrange("p t (c i) -> p c t i", i=4),
+                op=ALU.subtract,
+            )
+        for h in range(HALVES):
+            nc.vector.tensor_scalar_max(hid[h][:], pre[h][:], 0.0)
+        for h in range(HALVES):
+            nc.vector.quantize_mx(out=h_codes[h][:].bitcast(E5M2), scales=h_scales[h][:], in_=hid[h][:])
+            nc.tensor.matmul_mx(
+                out=p_ps[h][:], lhsT=h_codes[h][:].bitcast(E5M2), lhsT_scale=h_scales[h][:],
+                rhs=wb_codes[:].bitcast(E4M3), rhs_scale=wbs_sb[:], start=True, stop=True,
+            )
+            nc.scalar.activation(mag[h][:], p_ps[h][:], ACT.Abs)
+        for h in range(HALVES):
+            nc.vector.tensor_scalar(
+                out=mag[h][:], in0=mag[h][:], scalar1=0.2, scalar2=None, op0=ALU.add, op1=ALU.max, accum_out=den[h][:]
+            )
+        for h in range(HALVES):
+            nc.vector.reciprocal(inv[h][:], den[h][:])
+        for h in range(HALVES):
+            nc.vector.scalar_tensor_tensor(
+                out=res[h][:], in0=p_ps[h][:], scalar=inv[h][:], in1=rs_scaled[:, h, :], op0=ALU.mult, op1=ALU.add
+            )
+            nc.sync.dma_start(out=out[h * P : (h + 1) * P, :], in_=res[h][:])

@@ -55,34 +55,43 @@ def tile_list_boundedgaps_overtable_rowpeaks_kernel(
             nc.sync.dma_start(out=tile[:], in_=view[:, t0:t1, :])
             return [tile[:, t - t0, :] for t in range(t0, t1)]
 
-        nc.scalar.dma_start(out=hb_sb[:], in_=hb.rearrange("(a p t) o -> p a (t o)", a=PASSES, p=P, t=PACK))
+        nc.vector.memset(ws_raw[:].bitcast(I32), 0)
+        nc.vector.memset(wbs_sb[:].bitcast(I32), 0)
+        xb_planes = [load_planes("xb00", xb_v[0], 0, 2)]
         nc.scalar.dma_start(out=fk_sb[:], in_=fk.rearrange("(a p t) o -> p a (t o)", a=PASSES, p=P, t=PACK))
+        nc.scalar.dma_start(out=hb_sb[:], in_=hb.rearrange("(a p t) o -> p a (t o)", a=PASSES, p=P, t=PACK))
         nc.sync.dma_start(list_b[:], offs2)
-        xb_planes = [load_planes("xb0", xb_v[0], 0, 4)]
         nc.sync.dma_start(list_a[:], offs)
+        xa_planes = [load_planes("xa00", xa_v[0], 0, 2)]
+        xb_planes[0].extend(load_planes("xb02", xb_v[0], 2, 4))
+        xa_planes[0].extend(load_planes("xa02", xa_v[0], 2, 4))
         nc.sync.dma_start(out=w_raw[:].bitcast(I32), in_=w_words.rearrange("a p c -> p a c").bitcast(I32))
-        xa_planes = [load_planes("xa00", xa_v[0], 0, 2) + load_planes("xa02", xa_v[0], 2, 4)]
-        nc.sync.dma_start(list_t[:], offs3)
-        xb_planes.append(load_planes("xb1", xb_v[1], 0, 4))
-        xa_planes.append(
-            load_planes("xa10", xa_v[1], 0, 2) + load_planes("xa12", xa_v[1], 2, 3) + load_planes("xa13", xa_v[1], 3, 4)
-        )
-        tb_planes = load_planes("tb0", tb_v, 0, 2) + load_planes("tb2", tb_v, 2, 3) + load_planes("tb3", tb_v, 3, 4)
-        nc.sync.dma_start(out=wb_codes[:].bitcast(I32), in_=wb_words[0].rearrange("p n t -> p (n t)").bitcast(I32))
-        nc.sync.dma_start(out=rs_sb[:], in_=rs.rearrange("(h p) n -> p h n", p=P))
-
-        nc.gpsimd.memset(ws_raw[:].bitcast(I32), 0)
-        nc.gpsimd.memset(wbs_sb[:].bitcast(I32), 0)
         for q in range(4):
-            nc.gpsimd.dma_start(
+            nc.sync.dma_start(
                 out=ws_raw[32 * q : 32 * q + 4, :, :].bitcast(I32),
                 in_=w_scales[:, 4 * q : 4 * q + 4, :].rearrange("a r c -> r a c").bitcast(I32),
             )
+        nc.sync.dma_start(list_t[:], offs3)
+        xb_planes.append(load_planes("xb10", xb_v[1], 0, 2))
+        xa_planes.append(load_planes("xa10", xa_v[1], 0, 1) + load_planes("xa11", xa_v[1], 1, 2))
+        xb_planes[1].extend(load_planes("xb12", xb_v[1], 2, 3))
+        xa_planes[1].extend(load_planes("xa12", xa_v[1], 2, 3))
+        xb_planes[1].extend(load_planes("xb13", xb_v[1], 3, 4))
+        tb_planes = load_planes("tb0", tb_v, 0, 1)
+        xa_last = keep.tile([P, T], F32, name="xa_last")
+        nc.sync.dma_start(out=xa_last[:], in_=xa_v[PASSES - 1][:, PACK - 1, :])
+        for t in range(1, PACK):
+            tb_planes.extend(load_planes("tb%d" % t, tb_v, t, t + 1))
+        nc.sync.dma_start(out=wb_codes[:].bitcast(I32), in_=wb_words[0].rearrange("p n t -> p (n t)").bitcast(I32))
         for q in range(4):
-            nc.gpsimd.dma_start(
+            nc.sync.dma_start(
                 out=wbs_sb[32 * q : 32 * q + 4, :].bitcast(I32),
                 in_=wb_scales[0, 4 * q : 4 * q + 4, :].bitcast(I32),
             )
+        nc.sync.dma_start(out=rs_sb[:], in_=rs.rearrange("(h p) n -> p h n", p=P))
+
+        neg_fk = keep.tile([P, PASSES, PACK], F32, name="neg_fk")
+        nc.scalar.activation(neg_fk[:], fk_sb[:], ACT.Copy, scale=-1.0)
 
         nc.vector.tensor_copy(
             out=w_codes[:].bitcast(U16).rearrange("p a (t m) -> p a t m", t=PACK),
@@ -93,15 +102,16 @@ def tile_list_boundedgaps_overtable_rowpeaks_kernel(
             in_=ws_raw[:].rearrange("p a (m t) -> p a t m", t=PACK),
         )
 
-        def gather(dst, window, offsets, by_halves):
-            if by_halves:
-                for h in range(HALVES):
-                    part = offsets[:, h * HALF_COLS : (h + 1) * HALF_COLS]
-                    nc.scalar.activation(dst[:, h * P : (h + 1) * P], window.indirect(part), ACT.Copy)
-            else:
-                nc.scalar.activation(dst, window.indirect(offsets[:]), ACT.Copy)
+        halves = [slice(h * P, (h + 1) * P) for h in range(HALVES)]
+
+        def half_list(offsets, h):
+            return offsets[:, h * HALF_COLS : (h + 1) * HALF_COLS]
+
+        def gather(dst, window, offsets):
+            nc.scalar.activation(dst, window.indirect(offsets), ACT.Copy)
 
         a_ps = [psum.tile([P, PACK, P], F32, name="a_ps%d" % h) for h in range(HALVES)]
+        gt = keep.tile([P, PACK, J], F32, name="gt")
         for a in range(PASSES):
             ga = keep.tile([P, PACK, J], F32, name="ga%d" % a)
             gb = keep.tile([P, PACK, J], F32, name="gb%d" % a)
@@ -109,22 +119,33 @@ def tile_list_boundedgaps_overtable_rowpeaks_kernel(
             u_bf = keep.tile([P, J, PACK], BF16, name="u_bf%d" % a, align_bytes=64)
             u_codes = keep.tile([P, J], U32, name="u_codes%d" % a, align_bytes=64)
             u_scales = keep.tile([P, J], U8, name="u_scales%d" % a, align_bytes=64)
+
+            def neg_gap(t, js):
+                nc.vector.scalar_tensor_tensor(
+                    out=gap[:, t, js], in0=gb[:, t, js], scalar=hb_sb[:, a, t : t + 1], in1=ga[:, t, js],
+                    op0=ALU.min, op1=ALU.subtract,
+                )
+
+            def scale(t, js, factor):
+                nc.vector.tensor_scalar_mul(u_bf[:, js, t], gap[:, t, js], factor[:, a, t : t + 1])
+
             for t in range(PACK):
-                gather(gb[:, t, :], xb_planes[a][t], list_b, False)
-            for t in range(PACK):
-                last = a == PASSES - 1 and t == PACK - 1
-                gather(ga[:, t, :], xa_planes[a][t], list_a, last)
-                spans = [slice(h * P, (h + 1) * P) for h in range(HALVES)] if last else [slice(0, J)]
-                for js in spans:
-                    nc.vector.scalar_tensor_tensor(
-                        out=gap[:, t, js], in0=gb[:, t, js], scalar=hb_sb[:, a, t : t + 1], in1=ga[:, t, js],
-                        op0=ALU.min, op1=ALU.subtract,
+                gather(gb[:, t, :], xb_planes[a][t], list_b[:])
+                if a < PASSES - 1 or t < PACK - 1:
+                    gather(ga[:, t, :], xa_planes[a][t], list_a[:])
+                    neg_gap(t, slice(0, J))
+                    scale(t, slice(0, J), neg_fk)
+                else:
+                    gather(gt[:, 0, :], tb_planes[0], list_t[:])
+                    bounded = keep.tile([P, P], F32, name="bounded")
+                    nc.vector.tensor_scalar_min(bounded[:], gb[:, t, halves[0]], hb_sb[:, a, t : t + 1])
+                    gather(ga[:, t, halves[1]], xa_last[:], half_list(list_a, 1))
+                    nc.vector.tensor_tensor(
+                        gap[:, t, halves[0]], xa_last[:].indirect(half_list(list_a, 0)), bounded[:], ALU.subtract
                     )
-                for js in spans:
-                    nc.vector.tensor_scalar(
-                        out=u_bf[:, js, t], in0=gap[:, t, js], scalar1=fk_sb[:, a, t : t + 1], scalar2=-1.0,
-                        op0=ALU.mult, op1=ALU.mult,
-                    )
+                    neg_gap(t, halves[1])
+                    scale(t, halves[0], fk_sb)
+                    scale(t, halves[1], neg_fk)
             for h in range(HALVES):
                 js = slice(h * P, (h + 1) * P)
                 nc.vector.quantize_mx(
@@ -144,9 +165,10 @@ def tile_list_boundedgaps_overtable_rowpeaks_kernel(
                         stop=(a == PASSES - 1 and t == PACK - 1),
                     )
 
-        gt = keep.tile([P, PACK, J], F32, name="gt")
-        for t in range(PACK):
-            gather(gt[:, t, :], tb_planes[t], list_t, t == PACK - 1)
+        gather(gt[:, 1, :], tb_planes[1], list_t[:])
+        for t in range(2, PACK):
+            gather(gt[:, t, halves[0]], tb_planes[t], half_list(list_t, 0))
+            nc.vector.tensor_copy(gt[:, t, halves[1]], tb_planes[t].indirect(half_list(list_t, 1)))
         rs_scaled = keep.tile([P, HALVES, N], F32, name="rs_scaled")
         nc.scalar.activation(rs_scaled[:], rs_sb[:], ACT.Copy, scale=0.3)
 

@@ -21,8 +21,10 @@ P = 128
 PACK = 4
 PASSES = K // (P * PACK)
 HALVES = J // P
+QUADRANTS = 4
 LIST_COLS = J // 16
 HALF_COLS = P // 16
+RUN = 4
 
 
 def tile_list_boundedgaps_overtable_rowpeaks_kernel(
@@ -36,6 +38,11 @@ def tile_list_boundedgaps_overtable_rowpeaks_kernel(
         xa_v = xa.rearrange("(a p t) c -> a p t c", a=PASSES, p=P, t=PACK)
         xb_v = xb.rearrange("(a p t) c -> a p t c", a=PASSES, p=P, t=PACK)
         tb_v = tb.rearrange("(p t) c -> p t c", p=P, t=PACK)
+        halves = [slice(h * P, (h + 1) * P) for h in range(HALVES)]
+        all_slots = slice(0, J)
+
+        def per_half(name, shape, dtype):
+            return [keep.tile(shape, dtype, name="%s_%d" % (name, h), align_bytes=64) for h in range(HALVES)]
 
         list_a = keep.tile([P, LIST_COLS], U16, name="list_a")
         list_b = keep.tile([P, LIST_COLS], U16, name="list_b")
@@ -51,160 +58,195 @@ def tile_list_boundedgaps_overtable_rowpeaks_kernel(
         rs_sb = keep.tile([P, HALVES, N], F32, name="rs_sb")
 
         def load_planes(name, view, t0, t1):
-            tile = keep.tile([P, t1 - t0, view.shape[2]], F32, name=name)
-            nc.sync.dma_start(out=tile[:], in_=view[:, t0:t1, :])
-            return [tile[:, t - t0, :] for t in range(t0, t1)]
+            width = view.shape[2]
+            tile = keep.tile([P, (t1 - t0) * width], F32, name=name)
+            nc.sync.dma_start(out=tile[:], in_=view[:, t0:t1, :].rearrange("p t c -> p (t c)"))
+            return [tile[:, i * width : (i + 1) * width] for i in range(t1 - t0)]
 
         nc.vector.memset(ws_raw[:].bitcast(I32), 0)
         nc.vector.memset(wbs_sb[:].bitcast(I32), 0)
-        xb_planes = [load_planes("xb00", xb_v[0], 0, 2)]
+
+        xb_planes = [load_planes("xb0", xb_v[0], 0, 4)]
         nc.scalar.dma_start(out=fk_sb[:], in_=fk.rearrange("(a p t) o -> p a (t o)", a=PASSES, p=P, t=PACK))
         nc.scalar.dma_start(out=hb_sb[:], in_=hb.rearrange("(a p t) o -> p a (t o)", a=PASSES, p=P, t=PACK))
         nc.sync.dma_start(list_b[:], offs2)
         nc.sync.dma_start(list_a[:], offs)
-        xa_planes = [load_planes("xa00", xa_v[0], 0, 2)]
-        xb_planes[0].extend(load_planes("xb02", xb_v[0], 2, 4))
-        xa_planes[0].extend(load_planes("xa02", xa_v[0], 2, 4))
         nc.sync.dma_start(out=w_raw[:].bitcast(I32), in_=w_words.rearrange("a p c -> p a c").bitcast(I32))
-        for q in range(4):
+        xa_planes = [load_planes("xa00", xa_v[0], 0, 2)]
+        for q in range(QUADRANTS):
             nc.sync.dma_start(
                 out=ws_raw[32 * q : 32 * q + 4, :, :].bitcast(I32),
                 in_=w_scales[:, 4 * q : 4 * q + 4, :].rearrange("a r c -> r a c").bitcast(I32),
             )
-        nc.sync.dma_start(list_t[:], offs3)
+        xa_planes[0].extend(load_planes("xa02", xa_v[0], 2, 4))
         xb_planes.append(load_planes("xb10", xb_v[1], 0, 2))
         xa_planes.append(load_planes("xa10", xa_v[1], 0, 1) + load_planes("xa11", xa_v[1], 1, 2))
-        xb_planes[1].extend(load_planes("xb12", xb_v[1], 2, 3))
+        nc.sync.dma_start(list_t[:], offs3)
+        xb_planes[1].extend(load_planes("xb12", xb_v[1], 2, 4))
         xa_planes[1].extend(load_planes("xa12", xa_v[1], 2, 3))
-        xb_planes[1].extend(load_planes("xb13", xb_v[1], 3, 4))
         tb_planes = load_planes("tb0", tb_v, 0, 1)
-        xa_last = keep.tile([P, T], F32, name="xa_last")
-        nc.sync.dma_start(out=xa_last[:], in_=xa_v[PASSES - 1][:, PACK - 1, :])
+        xa_planes[1].extend(load_planes("xa13", xa_v[1], 3, 4))
         for t in range(1, PACK):
             tb_planes.extend(load_planes("tb%d" % t, tb_v, t, t + 1))
         nc.sync.dma_start(out=wb_codes[:].bitcast(I32), in_=wb_words[0].rearrange("p n t -> p (n t)").bitcast(I32))
-        for q in range(4):
+        nc.sync.dma_start(out=rs_sb[:], in_=rs.rearrange("(h p) n -> p h n", p=P))
+        for q in range(QUADRANTS):
             nc.sync.dma_start(
                 out=wbs_sb[32 * q : 32 * q + 4, :].bitcast(I32),
                 in_=wb_scales[0, 4 * q : 4 * q + 4, :].bitcast(I32),
             )
-        nc.sync.dma_start(out=rs_sb[:], in_=rs.rearrange("(h p) n -> p h n", p=P))
 
         neg_fk = keep.tile([P, PASSES, PACK], F32, name="neg_fk")
         nc.scalar.activation(neg_fk[:], fk_sb[:], ACT.Copy, scale=-1.0)
 
-        nc.vector.tensor_copy(
-            out=w_codes[:].bitcast(U16).rearrange("p a (t m) -> p a t m", t=PACK),
-            in_=w_raw[:].bitcast(U16).rearrange("p a (m t) -> p a t m", t=PACK),
-        )
-        nc.vector.tensor_copy(
-            out=ws_sb[:].rearrange("p a (t m) -> p a t m", t=PACK),
-            in_=ws_raw[:].rearrange("p a (m t) -> p a t m", t=PACK),
-        )
-
-        halves = [slice(h * P, (h + 1) * P) for h in range(HALVES)]
-
         def half_list(offsets, h):
             return offsets[:, h * HALF_COLS : (h + 1) * HALF_COLS]
 
-        def gather(dst, window, offsets):
+        def scalar_gather(dst, window, offsets):
             nc.scalar.activation(dst, window.indirect(offsets), ACT.Copy)
 
+        def deal_w():
+            nc.vector.tensor_copy(
+                out=w_codes[:].bitcast(U16).rearrange("p a (t m) -> p a t m", t=PACK),
+                in_=w_raw[:].bitcast(U16).rearrange("p a (m t) -> p a t m", t=PACK),
+            )
+            nc.vector.tensor_copy(
+                out=ws_sb[:].rearrange("p a (t m) -> p a t m", t=PACK),
+                in_=ws_raw[:].rearrange("p a (m t) -> p a t m", t=PACK),
+            )
+
         a_ps = [psum.tile([P, PACK, P], F32, name="a_ps%d" % h) for h in range(HALVES)]
-        gt = keep.tile([P, PACK, J], F32, name="gt")
+        tb_picked = per_half("tb_picked", [P, PACK, P], F32)
+
+        def gather_tb(t):
+            for h in range(HALVES):
+                scalar_gather(tb_picked[h][:, t, :], tb_planes[t], half_list(list_t, h))
+
         for a in range(PASSES):
-            ga = keep.tile([P, PACK, J], F32, name="ga%d" % a)
-            gb = keep.tile([P, PACK, J], F32, name="gb%d" % a)
+            last_pass = a == PASSES - 1
+            xa_picked = keep.tile([P, PACK, J], F32, name="xa_picked%d" % a)
+            xb_picked = keep.tile([P, PACK, J], F32, name="xb_picked%d" % a)
             gap = keep.tile([P, PACK, J], F32, name="gap%d" % a)
-            u_bf = keep.tile([P, J, PACK], BF16, name="u_bf%d" % a, align_bytes=64)
-            u_codes = keep.tile([P, J], U32, name="u_codes%d" % a, align_bytes=64)
-            u_scales = keep.tile([P, J], U8, name="u_scales%d" % a, align_bytes=64)
+            u_woven = per_half("u_woven%d" % a, [P, P, PACK], BF16)
+            u_codes = per_half("u_codes%d" % a, [P, P], U32)
+            u_scales = per_half("u_scales%d" % a, [P, P], U8)
 
-            def neg_gap(t, js):
+            def negated_gap(t, slots):
                 nc.vector.scalar_tensor_tensor(
-                    out=gap[:, t, js], in0=gb[:, t, js], scalar=hb_sb[:, a, t : t + 1], in1=ga[:, t, js],
-                    op0=ALU.min, op1=ALU.subtract,
+                    out=gap[:, t, slots], in0=xb_picked[:, t, slots], scalar=hb_sb[:, a, t : t + 1],
+                    in1=xa_picked[:, t, slots], op0=ALU.min, op1=ALU.subtract,
                 )
 
-            def scale(t, js, factor):
-                nc.vector.tensor_scalar_mul(u_bf[:, js, t], gap[:, t, js], factor[:, a, t : t + 1])
+            def gather_xb(t):
+                scalar_gather(xb_picked[:, t, :], xb_planes[a][t], list_b[:])
 
-            for t in range(PACK):
-                gather(gb[:, t, :], xb_planes[a][t], list_b[:])
-                if a < PASSES - 1 or t < PACK - 1:
-                    gather(ga[:, t, :], xa_planes[a][t], list_a[:])
-                    neg_gap(t, slice(0, J))
-                    scale(t, slice(0, J), neg_fk)
-                else:
-                    gather(gt[:, 0, :], tb_planes[0], list_t[:])
-                    bounded = keep.tile([P, P], F32, name="bounded")
-                    nc.vector.tensor_scalar_min(bounded[:], gb[:, t, halves[0]], hb_sb[:, a, t : t + 1])
-                    gather(ga[:, t, halves[1]], xa_last[:], half_list(list_a, 1))
+            def whole_plane(t):
+                scalar_gather(xa_picked[:, t, :], xa_planes[a][t], list_a[:])
+                negated_gap(t, all_slots)
+
+            def weave(planes):
+                for h in range(HALVES):
                     nc.vector.tensor_tensor(
-                        gap[:, t, halves[0]], xa_last[:].indirect(half_list(list_a, 0)), bounded[:], ALU.subtract
+                        out=u_woven[h][:, :, 0:planes].rearrange("p (c i) t -> p c t i", i=RUN),
+                        in0=gap[:, 0:planes, halves[h]].rearrange("p t (c i) -> p c t i", i=RUN),
+                        in1=neg_fk[:, a, 0:planes].unsqueeze(1).unsqueeze(3).to_broadcast([P, P // RUN, planes, RUN]),
+                        op=ALU.mult,
                     )
-                    neg_gap(t, halves[1])
-                    scale(t, halves[0], fk_sb)
-                    scale(t, halves[1], neg_fk)
+
+            def bound_first_half(t):
+                bounded = keep.tile([P, P], F32, name="bounded%d" % t)
+                nc.vector.tensor_scalar_min(bounded[:], xb_picked[:, t, halves[0]], hb_sb[:, a, t : t + 1])
+                return bounded
+
+            def shared_plane(t, bounded):
+                scalar_gather(xa_picked[:, t, halves[1]], xa_planes[a][t], half_list(list_a, 1))
+                nc.vector.tensor_tensor(
+                    gap[:, t, halves[0]], xa_planes[a][t].indirect(half_list(list_a, 0)), bounded[:], ALU.subtract
+                )
+                negated_gap(t, halves[1])
+                for h, factor in enumerate((fk_sb, neg_fk)):
+                    nc.vector.tensor_scalar_mul(u_woven[h][:, :, t], gap[:, t, halves[h]], factor[:, a, t : t + 1])
+
+            if not last_pass:
+                for t in range(PACK):
+                    gather_xb(t)
+                deal_w()
+                for t in range(PACK):
+                    whole_plane(t)
+                weave(PACK)
+            else:
+                for t in (0, 1):
+                    gather_xb(t)
+                for t in (0, 1):
+                    whole_plane(t)
+                weave(2)
+                gather_xb(2)
+                bounded = bound_first_half(2)
+                gather_xb(3)
+                shared_plane(2, bounded)
+                bounded = bound_first_half(3)
+                gather_tb(0)
+                shared_plane(3, bounded)
             for h in range(HALVES):
-                js = slice(h * P, (h + 1) * P)
                 nc.vector.quantize_mx(
-                    out=u_codes[:, js].bitcast(E4M3), scales=u_scales[:, js],
-                    in_=u_bf[:, js, :].rearrange("p j t -> p (j t)"),
+                    out=u_codes[h][:].bitcast(E4M3), scales=u_scales[h][:],
+                    in_=u_woven[h][:].rearrange("p j t -> p (j t)"),
                 )
             for h in range(HALVES):
-                js = slice(h * P, (h + 1) * P)
                 for t in range(PACK):
                     nc.tensor.matmul_mx(
                         out=a_ps[h][:, t, :],
                         lhsT=w_codes[:, a, 2 * P * t : 2 * P * (t + 1)].bitcast(E2M1),
                         lhsT_scale=ws_sb[:, a, P * t : P * (t + 1)],
-                        rhs=u_codes[:, js].bitcast(E4M3),
-                        rhs_scale=u_scales[:, js],
+                        rhs=u_codes[h][:].bitcast(E4M3),
+                        rhs_scale=u_scales[h][:],
                         start=(a == 0 and t == 0),
-                        stop=(a == PASSES - 1 and t == PACK - 1),
+                        stop=(last_pass and t == PACK - 1),
                     )
 
-        gather(gt[:, 1, :], tb_planes[1], list_t[:])
-        for t in range(2, PACK):
-            gather(gt[:, t, halves[0]], tb_planes[t], half_list(list_t, 0))
-            nc.vector.tensor_copy(gt[:, t, halves[1]], tb_planes[t].indirect(half_list(list_t, 1)))
+        gather_tb(1)
+        for t in (2, 3):
+            scalar_gather(tb_picked[0][:, t, :], tb_planes[t], half_list(list_t, 0))
+        nc.vector.tensor_copy(tb_picked[1][:, 2, :], tb_planes[2].indirect(half_list(list_t, 1)))
+        scalar_gather(tb_picked[1][:, 3, :], tb_planes[3], half_list(list_t, 1))
         rs_scaled = keep.tile([P, HALVES, N], F32, name="rs_scaled")
         nc.scalar.activation(rs_scaled[:], rs_sb[:], ACT.Copy, scale=0.3)
 
-        pre = [keep.tile([P, P * PACK], BF16, name="pre%d" % h, align_bytes=64) for h in range(HALVES)]
-        hid = [keep.tile([P, P * PACK], BF16, name="hid%d" % h, align_bytes=64) for h in range(HALVES)]
-        h_codes = [keep.tile([P, P], U32, name="h_codes%d" % h, align_bytes=64) for h in range(HALVES)]
-        h_scales = [keep.tile([P, P], U8, name="h_scales%d" % h, align_bytes=64) for h in range(HALVES)]
+        diff = per_half("diff", [P, P * PACK], BF16)
+        hid = per_half("hid", [P, P * PACK], BF16)
+        hid_codes = per_half("hid_codes", [P, P], U32)
+        hid_scales = per_half("hid_scales", [P, P], U8)
         p_ps = [psum.tile([P, N], F32, name="p_ps%d" % h) for h in range(HALVES)]
-        mag = [keep.tile([P, N], F32, name="mag%d" % h) for h in range(HALVES)]
-        den = [keep.tile([P, 1], F32, name="den%d" % h) for h in range(HALVES)]
-        inv = [keep.tile([P, 1], F32, name="inv%d" % h) for h in range(HALVES)]
-        res = [keep.tile([P, N], F32, name="res%d" % h) for h in range(HALVES)]
+        magnitude = per_half("magnitude", [P, N], F32)
+        divisor = per_half("divisor", [P, 1], F32)
+        inverse = per_half("inverse", [P, 1], F32)
+        result = per_half("result", [P, N], F32)
         for h in range(HALVES):
             nc.vector.tensor_tensor(
-                out=pre[h][:].rearrange("p (c i t) -> p c t i", i=4, t=PACK),
-                in0=a_ps[h][:].rearrange("p t (c i) -> p c t i", i=4),
-                in1=gt[:, :, h * P : (h + 1) * P].rearrange("p t (c i) -> p c t i", i=4),
+                out=diff[h][:].rearrange("p (c i t) -> p c t i", i=RUN, t=PACK),
+                in0=a_ps[h][:].rearrange("p t (c i) -> p c t i", i=RUN),
+                in1=tb_picked[h][:].rearrange("p t (c i) -> p c t i", i=RUN),
                 op=ALU.subtract,
             )
         for h in range(HALVES):
-            nc.vector.tensor_scalar_max(hid[h][:], pre[h][:], 0.0)
+            nc.vector.tensor_scalar_max(hid[h][:], diff[h][:], 0.0)
         for h in range(HALVES):
-            nc.vector.quantize_mx(out=h_codes[h][:].bitcast(E5M2), scales=h_scales[h][:], in_=hid[h][:])
+            nc.vector.quantize_mx(out=hid_codes[h][:].bitcast(E5M2), scales=hid_scales[h][:], in_=hid[h][:])
             nc.tensor.matmul_mx(
-                out=p_ps[h][:], lhsT=h_codes[h][:].bitcast(E5M2), lhsT_scale=h_scales[h][:],
+                out=p_ps[h][:], lhsT=hid_codes[h][:].bitcast(E5M2), lhsT_scale=hid_scales[h][:],
                 rhs=wb_codes[:].bitcast(E4M3), rhs_scale=wbs_sb[:], start=True, stop=True,
             )
-            nc.scalar.activation(mag[h][:], p_ps[h][:], ACT.Abs)
+            nc.scalar.activation(magnitude[h][:], p_ps[h][:], ACT.Abs)
         for h in range(HALVES):
             nc.vector.tensor_scalar(
-                out=mag[h][:], in0=mag[h][:], scalar1=0.2, scalar2=None, op0=ALU.add, op1=ALU.max, accum_out=den[h][:]
+                out=magnitude[h][:], in0=magnitude[h][:], scalar1=0.2, scalar2=None,
+                op0=ALU.add, op1=ALU.max, accum_out=divisor[h][:],
             )
         for h in range(HALVES):
-            nc.vector.reciprocal(inv[h][:], den[h][:])
+            nc.vector.reciprocal(inverse[h][:], divisor[h][:])
         for h in range(HALVES):
             nc.vector.scalar_tensor_tensor(
-                out=res[h][:], in0=p_ps[h][:], scalar=inv[h][:], in1=rs_scaled[:, h, :], op0=ALU.mult, op1=ALU.add
+                out=result[h][:], in0=p_ps[h][:], scalar=inverse[h][:], in1=rs_scaled[:, h, :],
+                op0=ALU.mult, op1=ALU.add,
             )
-            nc.sync.dma_start(out=out[h * P : (h + 1) * P, :], in_=res[h][:])
+            nc.sync.dma_start(out=out[halves[h], :], in_=result[h][:])

from contextlib import ExitStack

import concourse.mybir as mybir

K, T, J, S, R, V, N = 1024, 1024, 256, 512, 512, 512, 256
FLOPS = 2 * K * R * J + 2 * R * J * N

F32 = mybir.dt.float32
BF16 = mybir.dt.bfloat16
I32 = mybir.dt.int32
U32 = mybir.dt.uint32
U16 = mybir.dt.uint16
U8 = mybir.dt.uint8
E4M3 = mybir.dt.float8_e4m3fn_x4
E5M2 = mybir.dt.float8_e5m2_x4
E2M1 = mybir.dt.float4_e2m1fn_x4
ALU = mybir.AluOpType
ACT = mybir.ActivationFunctionType

P = 128
PACK = 4
PASSES = K // (P * PACK)
HALVES = J // P
QUADRANTS = 4
LIST_COLS = J // 16
HALF_COLS = P // 16
RUN = 4


def tile_list_boundedgaps_overtable_rowpeaks_kernel(
    tc, xa, xb, hb, fk, w_words, w_scales, tb, wb_words, wb_scales, rs, offs, offs2, offs3, out
):
    nc = tc.nc
    with ExitStack() as ctx:
        keep = ctx.enter_context(tc.tile_pool(name="keep", bufs=1))
        psum = ctx.enter_context(tc.psum_pool(name="psum", bufs=1))

        xa_v = xa.rearrange("(a p t) c -> a p t c", a=PASSES, p=P, t=PACK)
        xb_v = xb.rearrange("(a p t) c -> a p t c", a=PASSES, p=P, t=PACK)
        tb_v = tb.rearrange("(p t) c -> p t c", p=P, t=PACK)
        halves = [slice(h * P, (h + 1) * P) for h in range(HALVES)]
        all_slots = slice(0, J)

        def per_half(name, shape, dtype):
            return [keep.tile(shape, dtype, name="%s_%d" % (name, h), align_bytes=64) for h in range(HALVES)]

        list_a = keep.tile([P, LIST_COLS], U16, name="list_a")
        list_b = keep.tile([P, LIST_COLS], U16, name="list_b")
        list_t = keep.tile([P, LIST_COLS], U16, name="list_t")
        hb_sb = keep.tile([P, PASSES, PACK], F32, name="hb_sb")
        fk_sb = keep.tile([P, PASSES, PACK], F32, name="fk_sb")
        w_raw = keep.tile([P, PASSES, 2 * R], U8, name="w_raw", align_bytes=64)
        w_codes = keep.tile([P, PASSES, 2 * R], U8, name="w_codes", align_bytes=64)
        ws_raw = keep.tile([P, PASSES, R], U8, name="ws_raw", align_bytes=64)
        ws_sb = keep.tile([P, PASSES, R], U8, name="ws_sb", align_bytes=64)
        wb_codes = keep.tile([P, N], U32, name="wb_codes", align_bytes=64)
        wbs_sb = keep.tile([P, N], U8, name="wbs_sb", align_bytes=64)
        rs_sb = keep.tile([P, HALVES, N], F32, name="rs_sb")

        def load_planes(name, view, t0, t1):
            width = view.shape[2]
            tile = keep.tile([P, (t1 - t0) * width], F32, name=name)
            nc.sync.dma_start(out=tile[:], in_=view[:, t0:t1, :].rearrange("p t c -> p (t c)"))
            return [tile[:, i * width : (i + 1) * width] for i in range(t1 - t0)]

        nc.vector.memset(ws_raw[:].bitcast(I32), 0)
        nc.vector.memset(wbs_sb[:].bitcast(I32), 0)

        xb_planes = [load_planes("xb0", xb_v[0], 0, 4)]
        nc.scalar.dma_start(out=fk_sb[:], in_=fk.rearrange("(a p t) o -> p a (t o)", a=PASSES, p=P, t=PACK))
        nc.scalar.dma_start(out=hb_sb[:], in_=hb.rearrange("(a p t) o -> p a (t o)", a=PASSES, p=P, t=PACK))
        nc.sync.dma_start(list_b[:], offs2)
        nc.sync.dma_start(list_a[:], offs)
        nc.sync.dma_start(out=w_raw[:].bitcast(I32), in_=w_words.rearrange("a p c -> p a c").bitcast(I32))
        xa_planes = [load_planes("xa00", xa_v[0], 0, 2)]
        for q in range(QUADRANTS):
            nc.sync.dma_start(
                out=ws_raw[32 * q : 32 * q + 4, :, :].bitcast(I32),
                in_=w_scales[:, 4 * q : 4 * q + 4, :].rearrange("a r c -> r a c").bitcast(I32),
            )
        xa_planes[0].extend(load_planes("xa02", xa_v[0], 2, 4))
        xb_planes.append(load_planes("xb10", xb_v[1], 0, 2))
        xa_planes.append(load_planes("xa10", xa_v[1], 0, 1) + load_planes("xa11", xa_v[1], 1, 2))
        nc.sync.dma_start(list_t[:], offs3)
        xb_planes[1].extend(load_planes("xb12", xb_v[1], 2, 4))
        xa_planes[1].extend(load_planes("xa12", xa_v[1], 2, 3))
        tb_planes = load_planes("tb0", tb_v, 0, 1)
        xa_planes[1].extend(load_planes("xa13", xa_v[1], 3, 4))
        for t in range(1, PACK):
            tb_planes.extend(load_planes("tb%d" % t, tb_v, t, t + 1))
        nc.sync.dma_start(out=wb_codes[:].bitcast(I32), in_=wb_words[0].rearrange("p n t -> p (n t)").bitcast(I32))
        nc.sync.dma_start(out=rs_sb[:], in_=rs.rearrange("(h p) n -> p h n", p=P))
        for q in range(QUADRANTS):
            nc.sync.dma_start(
                out=wbs_sb[32 * q : 32 * q + 4, :].bitcast(I32),
                in_=wb_scales[0, 4 * q : 4 * q + 4, :].bitcast(I32),
            )

        neg_fk = keep.tile([P, PASSES, PACK], F32, name="neg_fk")
        nc.scalar.activation(neg_fk[:], fk_sb[:], ACT.Copy, scale=-1.0)

        def half_list(offsets, h):
            return offsets[:, h * HALF_COLS : (h + 1) * HALF_COLS]

        def scalar_gather(dst, window, offsets):
            nc.scalar.activation(dst, window.indirect(offsets), ACT.Copy)

        def deal_w():
            nc.vector.tensor_copy(
                out=w_codes[:].bitcast(U16).rearrange("p a (t m) -> p a t m", t=PACK),
                in_=w_raw[:].bitcast(U16).rearrange("p a (m t) -> p a t m", t=PACK),
            )
            nc.vector.tensor_copy(
                out=ws_sb[:].rearrange("p a (t m) -> p a t m", t=PACK),
                in_=ws_raw[:].rearrange("p a (m t) -> p a t m", t=PACK),
            )

        a_ps = [psum.tile([P, PACK, P], F32, name="a_ps%d" % h) for h in range(HALVES)]
        tb_picked = per_half("tb_picked", [P, PACK, P], F32)

        def gather_tb(t):
            for h in range(HALVES):
                scalar_gather(tb_picked[h][:, t, :], tb_planes[t], half_list(list_t, h))

        for a in range(PASSES):
            last_pass = a == PASSES - 1
            xa_picked = keep.tile([P, PACK, J], F32, name="xa_picked%d" % a)
            xb_picked = keep.tile([P, PACK, J], F32, name="xb_picked%d" % a)
            gap = keep.tile([P, PACK, J], F32, name="gap%d" % a)
            u_woven = per_half("u_woven%d" % a, [P, P, PACK], BF16)
            u_codes = per_half("u_codes%d" % a, [P, P], U32)
            u_scales = per_half("u_scales%d" % a, [P, P], U8)

            def negated_gap(t, slots):
                nc.vector.scalar_tensor_tensor(
                    out=gap[:, t, slots], in0=xb_picked[:, t, slots], scalar=hb_sb[:, a, t : t + 1],
                    in1=xa_picked[:, t, slots], op0=ALU.min, op1=ALU.subtract,
                )

            def gather_xb(t):
                scalar_gather(xb_picked[:, t, :], xb_planes[a][t], list_b[:])

            def whole_plane(t):
                scalar_gather(xa_picked[:, t, :], xa_planes[a][t], list_a[:])
                negated_gap(t, all_slots)

            def weave(planes):
                for h in range(HALVES):
                    nc.vector.tensor_tensor(
                        out=u_woven[h][:, :, 0:planes].rearrange("p (c i) t -> p c t i", i=RUN),
                        in0=gap[:, 0:planes, halves[h]].rearrange("p t (c i) -> p c t i", i=RUN),
                        in1=neg_fk[:, a, 0:planes].unsqueeze(1).unsqueeze(3).to_broadcast([P, P // RUN, planes, RUN]),
                        op=ALU.mult,
                    )

            def bound_first_half(t):
                bounded = keep.tile([P, P], F32, name="bounded%d" % t)
                nc.vector.tensor_scalar_min(bounded[:], xb_picked[:, t, halves[0]], hb_sb[:, a, t : t + 1])
                return bounded

            def shared_plane(t, bounded):
                scalar_gather(xa_picked[:, t, halves[1]], xa_planes[a][t], half_list(list_a, 1))
                nc.vector.tensor_tensor(
                    gap[:, t, halves[0]], xa_planes[a][t].indirect(half_list(list_a, 0)), bounded[:], ALU.subtract
                )
                negated_gap(t, halves[1])
                for h, factor in enumerate((fk_sb, neg_fk)):
                    nc.vector.tensor_scalar_mul(u_woven[h][:, :, t], gap[:, t, halves[h]], factor[:, a, t : t + 1])

            if not last_pass:
                for t in range(PACK):
                    gather_xb(t)
                deal_w()
                for t in range(PACK):
                    whole_plane(t)
                weave(PACK)
            else:
                for t in (0, 1):
                    gather_xb(t)
                for t in (0, 1):
                    whole_plane(t)
                weave(2)
                gather_xb(2)
                bounded = bound_first_half(2)
                gather_xb(3)
                shared_plane(2, bounded)
                bounded = bound_first_half(3)
                gather_tb(0)
                shared_plane(3, bounded)
            for h in range(HALVES):
                nc.vector.quantize_mx(
                    out=u_codes[h][:].bitcast(E4M3), scales=u_scales[h][:],
                    in_=u_woven[h][:].rearrange("p j t -> p (j t)"),
                )
            for h in range(HALVES):
                for t in range(PACK):
                    nc.tensor.matmul_mx(
                        out=a_ps[h][:, t, :],
                        lhsT=w_codes[:, a, 2 * P * t : 2 * P * (t + 1)].bitcast(E2M1),
                        lhsT_scale=ws_sb[:, a, P * t : P * (t + 1)],
                        rhs=u_codes[h][:].bitcast(E4M3),
                        rhs_scale=u_scales[h][:],
                        start=(a == 0 and t == 0),
                        stop=(last_pass and t == PACK - 1),
                    )

        gather_tb(1)
        for t in (2, 3):
            scalar_gather(tb_picked[0][:, t, :], tb_planes[t], half_list(list_t, 0))
        nc.vector.tensor_copy(tb_picked[1][:, 2, :], tb_planes[2].indirect(half_list(list_t, 1)))
        scalar_gather(tb_picked[1][:, 3, :], tb_planes[3], half_list(list_t, 1))
        rs_scaled = keep.tile([P, HALVES, N], F32, name="rs_scaled")
        nc.scalar.activation(rs_scaled[:], rs_sb[:], ACT.Copy, scale=0.3)

        diff = per_half("diff", [P, P * PACK], BF16)
        hid = per_half("hid", [P, P * PACK], BF16)
        hid_codes = per_half("hid_codes", [P, P], U32)
        hid_scales = per_half("hid_scales", [P, P], U8)
        p_ps = [psum.tile([P, N], F32, name="p_ps%d" % h) for h in range(HALVES)]
        magnitude = per_half("magnitude", [P, N], F32)
        divisor = per_half("divisor", [P, 1], F32)
        inverse = per_half("inverse", [P, 1], F32)
        result = per_half("result", [P, N], F32)
        for h in range(HALVES):
            nc.vector.tensor_tensor(
                out=diff[h][:].rearrange("p (c i t) -> p c t i", i=RUN, t=PACK),
                in0=a_ps[h][:].rearrange("p t (c i) -> p c t i", i=RUN),
                in1=tb_picked[h][:].rearrange("p t (c i) -> p c t i", i=RUN),
                op=ALU.subtract,
            )
        for h in range(HALVES):
            nc.vector.tensor_scalar_max(hid[h][:], diff[h][:], 0.0)
        for h in range(HALVES):
            nc.vector.quantize_mx(out=hid_codes[h][:].bitcast(E5M2), scales=hid_scales[h][:], in_=hid[h][:])
            nc.tensor.matmul_mx(
                out=p_ps[h][:], lhsT=hid_codes[h][:].bitcast(E5M2), lhsT_scale=hid_scales[h][:],
                rhs=wb_codes[:].bitcast(E4M3), rhs_scale=wbs_sb[:], start=True, stop=True,
            )
            nc.scalar.activation(magnitude[h][:], p_ps[h][:], ACT.Abs)
        for h in range(HALVES):
            nc.vector.tensor_scalar(
                out=magnitude[h][:], in0=magnitude[h][:], scalar1=0.2, scalar2=None,
                op0=ALU.add, op1=ALU.max, accum_out=divisor[h][:],
            )
        for h in range(HALVES):
            nc.vector.reciprocal(inverse[h][:], divisor[h][:])
        for h in range(HALVES):
            nc.vector.scalar_tensor_tensor(
                out=result[h][:], in0=p_ps[h][:], scalar=inverse[h][:], in1=rs_scaled[:, h, :],
                op0=ALU.mult, op1=ALU.add,
            )
            nc.sync.dma_start(out=out[halves[h], :], in_=result[h][:])
